import numpy as np
import ml_dtypes


def mxq(x, axis, fmt="e4m3"):
    dtype, down = {"e4m3": (ml_dtypes.float8_e4m3fn, 7), "e5m2": (ml_dtypes.float8_e5m2, 14)}[fmt]
    v = np.moveaxis(np.asarray(x, np.float32).astype(ml_dtypes.bfloat16).astype(np.float64), axis, -1)
    blocks = v.reshape(v.shape[:-1] + (-1, 32))
    amax = np.abs(blocks).max(-1, keepdims=True)
    byte = np.maximum(np.where(amax > 0, np.frexp(amax)[1] - 1 + 127, 0) - down, 1)
    scale = np.exp2(byte - 127.0)
    codes = (blocks / scale).astype(np.float32).astype(dtype).astype(np.float64)
    return np.moveaxis((codes * scale).reshape(v.shape), -1, axis)


WIDE = False


def mx_kscale(k):
    if not WIDE:
        return np.ones(k)
    levels = np.array([10, -10, 5, -5, 0])
    if k % 512:
        return np.exp2(np.random.permutation(np.resize(levels, k // 32))).repeat(32)
    a = np.empty((k // 512, 16))
    for p in range(k // 512):
        a[p, :8] = np.random.permutation(np.resize(levels, 8))
        for g in range(8):
            far = levels[np.abs(levels - a[p, g]) >= 10]
            a[p, g + 8] = far[np.random.randint(len(far))]
    return np.exp2(a.ravel()).repeat(32)


def f64(x):
    return np.asarray(x).astype(np.float64)


def striped(idx):
    return np.tile(idx.reshape(-1, 16).T, (8, 1)).astype(np.uint16)


def unstriped(offs):
    return offs[:16].T.reshape(-1).astype(np.int64)


def striped8(idx):
    return np.concatenate([x.reshape(-1, 16).T for x in idx]).astype(np.uint16)


def runs(offs, k):
    lists = np.stack([offs[16 * r : 16 * r + 16].T.reshape(-1) for r in range(8)]).astype(np.int64)
    return lists[np.arange(k) % 512 // 64]


def pack_weight(w):
    k, n = w.shape
    w = f64(np.asarray(w, np.float32).astype(ml_dtypes.bfloat16)).reshape(k // 32, 32, n)
    amax = np.abs(w).max(1)
    byte = np.clip(np.where(amax > 0, np.frexp(amax)[1] - 1 + 127 - 7, 1), 1, 254)
    scaled = (w * np.exp2(127.0 - byte)[:, None, :]).reshape(k, n).astype(np.float32)
    words = np.ascontiguousarray(scaled.reshape(k // 512, 128, 4, n).transpose(0, 1, 3, 2)).astype(ml_dtypes.float8_e4m3fn).view(np.uint8)
    return words, np.ascontiguousarray(byte.astype(np.uint8).reshape(k // 512, 16, n))


def unpack_weight(words, scales):
    g, p, n, _ = words.shape
    vals = np.ascontiguousarray(words).view(ml_dtypes.float8_e4m3fn).astype(np.float64) * np.repeat(np.exp2(scales.astype(np.float64) - 127.0), 8, axis=1)[..., None]
    return vals.transpose(0, 1, 3, 2).reshape(g * 512, n)


E2M1 = np.array([0.0, 0.5, 1.0, 1.5, 2.0, 3.0, 4.0, 6.0, -0.0, -0.5, -1.0, -1.5, -2.0, -3.0, -4.0, -6.0])


def pack_fp4(w):
    k, n = w.shape
    w = f64(np.asarray(w, np.float32).astype(ml_dtypes.bfloat16)).reshape(k // 32, 32, n)
    amax = np.abs(w).max(1)
    mant, ex = np.frexp(amax / 6.0)
    byte = np.clip(np.where(amax > 0, np.where(mant > 0.5, ex, ex - 1) + 127, 1), 1, 254)
    scaled = (w * np.exp2(127.0 - byte)[:, None, :]).reshape(k, n).astype(np.float32)
    c = np.ascontiguousarray(scaled.reshape(k // 512, 128, 4, n).transpose(0, 1, 3, 2)).astype(ml_dtypes.float4_e2m1fn).view(np.uint8) & 0xF
    words = (c[..., 0::2] | (c[..., 1::2] << 4)).reshape(k // 512, 128, 2 * n)
    return np.ascontiguousarray(words), np.ascontiguousarray(byte.astype(np.uint8).reshape(k // 512, 16, n))


def unpack_fp4(words, scales):
    g, _, n = scales.shape
    words = np.ascontiguousarray(words).reshape(g, 128, n, 2)
    nib = np.empty((g, 128, n, 4), np.uint8)
    nib[..., 0::2] = words & 0xF
    nib[..., 1::2] = words >> 4
    vals = E2M1[nib] * np.repeat(np.exp2(scales.astype(np.float64) - 127.0), 8, axis=1)[..., None]
    return vals.transpose(0, 1, 3, 2).reshape(g * 512, n)


def sigmoid(v):
    return 1.0 / (1.0 + np.exp(-np.maximum(v, -700.0)))

def planes(y):
    n, m = y.shape
    v = y.astype(np.float32).astype(ml_dtypes.bfloat16).astype(np.float64).reshape(n // 32, 32, m)
    top = np.abs(v).max(1)
    byte = np.clip(np.where(top > 0, np.frexp(top)[1] - 1 + 127 - 7, 1), 1, 254)
    codes = (v * np.exp2(127.0 - byte)[:, None, :]).reshape(n, m).astype(np.float32).astype(ml_dtypes.float8_e4m3fn).view(np.uint8)
    words = codes.reshape(n // 512, 128, 4, m).transpose(0, 1, 3, 2)
    return np.ascontiguousarray(words), np.ascontiguousarray(byte.astype(np.uint8).reshape(n // 512, 16, m))


K, T, S, H, W = 512, 2048, 512, 512, 256


def setup_inputs():
    n = np.random.standard_normal
    s = mx_kscale(K)[:, None]
    u = mx_kscale(H)
    packed_xT = pack_weight(n((K, T)) * s)
    packed_w1 = pack_fp4(n((K, H)) / np.sqrt(K) / s)
    packed_w2 = pack_fp4(n((H, H)) / np.sqrt(H) / u[:, None])
    perm = np.stack([np.random.permutation(S) for _ in range(8)])
    return {
        "x_words": packed_xT[0],
        "x_scales": packed_xT[1],
        "w1_words": packed_w1[0],
        "w1_scales": packed_w1[1],
        "gn": (np.random.uniform(0.5, 1.5, (H, 1)) * u[:, None]).astype(np.float32),
        "w2_words": packed_w2[0],
        "w2_scales": packed_w2[1],
        "offs": striped(np.random.permutation(T)[:S]),
        "n1": striped8(np.stack([np.random.permutation(S) for _ in range(8)])),
        "n2": striped8(np.stack([np.random.permutation(S) for _ in range(8)])),
        "n3": striped8(perm[:, :W]),
        "n4": striped8(perm[:, W:]),
        "n5": striped8(np.stack([np.random.permutation(S) for _ in range(8)])),
        "n6": striped8(np.stack([np.random.permutation(S) for _ in range(8)])),
    }


def reference(x_words, x_scales, w1_words, w1_scales, gn, w2_words, w2_scales, offs, n1, n2, n3, n4, n5, n6):
    xq = unpack_weight(x_words, x_scales)[:, unstriped(offs)]
    y = unpack_fp4(w1_words, w1_scales).T @ xq
    z = f64(gn) * (0.75 * (y[np.arange(H)[:, None], runs(n1, H)] + y[np.arange(H)[:, None], runs(n2, H)]) - y)
    w2q = unpack_fp4(w2_words, w2_scales)
    a = w2q.T @ mxq(z, 0, "e4m3")
    pb = y[np.arange(H)[:, None], runs(n4, H)]
    pa = y[np.arange(H)[:, None], runs(n3, H)]
    rb = pb * sigmoid(pb - pa)
    ra = pa * sigmoid(pa - pb)
    ds = np.zeros((H, S))
    ds[np.arange(H)[:, None], runs(n3, H)] = ra
    dt = ds.copy()
    dt[np.arange(H)[:, None], runs(n4, H)] = rb
    z2 = f64(gn) * dt
    b = w2q.T @ mxq(z2, 0, "e4m3")
    out_0 = (a - (a[np.arange(H)[:, None], runs(n5, H)])) / (np.abs(b) + np.abs(b[np.arange(H)[:, None], runs(n6, H)]) + 0.5)
    return (out_0,) + planes(out_0)

@@ -1,0 +1,278 @@
+from contextlib import ExitStack
+
+import concourse.mybir as mybir
+
+K, T, S, H, W = 512, 2048, 512, 512, 256
+FLOPS = 3 * 2 * 512 * 512 * 512
+
+F32 = mybir.dt.float32
+BF16 = mybir.dt.bfloat16
+I32 = mybir.dt.int32
+U32 = mybir.dt.uint32
+U16 = mybir.dt.uint16
+U8 = mybir.dt.uint8
+FP8X4 = mybir.dt.float8_e4m3fn_x4
+FP4X4 = mybir.dt.float4_e2m1fn_x4
+ACT = mybir.ActivationFunctionType
+ALU = mybir.AluOpType
+
+P = 128
+PACK = 4
+HALF = S // 2
+WIDE = 2 * S
+
+
+def tile_picked_tienormblapduel_none_po_kernel(
+    tc, x_words, x_scales, w1_words, w1_scales, gn, w2_words, w2_scales, offs, n1, n2, n3, n4, n5, n6, out_0, out_1, out_2
+):
+    nc = tc.nc
+    with ExitStack() as ctx:
+        lists = ctx.enter_context(tc.tile_pool(name="lists", bufs=1))
+        keep = ctx.enter_context(tc.tile_pool(name="keep", bufs=1))
+        psum = ctx.enter_context(tc.psum_pool(name="psum", bufs=1))
+
+        def load_list(src, name):
+            tile = lists.tile([P, src.shape[1]], U16, name=name)
+            nc.sync.dma_start(tile[:], src)
+            return tile
+
+        def cleared(src, name):
+            tile = keep.tile([P, src.shape[2]], U8, name=name, align_bytes=64)
+            nc.vector.memset(tile[:].bitcast(I32), 0)
+            return tile
+
+        def load_scale_rows(queues, tile, src):
+            for q in range(4):
+                queues[q].dma_start(tile[32 * q : 32 * q + 4, :].bitcast(I32), src[0, 4 * q : 4 * q + 4, :].bitcast(I32))
+
+        def load_weight_words(src, name):
+            tile = keep.tile([P, 2 * H], U8, name=name, align_bytes=64)
+            nc.sync.dma_start(tile[:].bitcast(I32), src[0].bitcast(I32))
+            return tile
+
+        def deal(words, scales, name):
+            dealt_words = keep.tile([P, 2 * H], U8, name=name + "_words", align_bytes=64)
+            dealt_scales = keep.tile([P, H], U8, name=name + "_scales", align_bytes=64)
+            nc.vector.tensor_copy(
+                dealt_words[:].rearrange("p (t m b) -> p t m b", t=PACK, b=2),
+                words[:].rearrange("p (m t b) -> p t m b", t=PACK, b=2),
+            )
+            nc.vector.tensor_copy(
+                dealt_scales[:].rearrange("p (t m) -> p t m", t=PACK),
+                scales[:].rearrange("p (m t) -> p t m", t=PACK),
+            )
+            return dealt_words, dealt_scales
+
+        def product(weight, codes, scales, t, tag):
+            bank = psum.tile([P, S], F32, name=tag + str(t), tag=tag + str(t))
+            nc.tensor.matmul_mx(
+                bank[:],
+                lhsT=weight[0][:, 2 * P * t : 2 * P * (t + 1)].bitcast(FP4X4),
+                lhsT_scale=weight[1][:, P * t : P * (t + 1)],
+                rhs=codes[:].bitcast(FP8X4),
+                rhs_scale=scales[:],
+                start=True,
+                stop=True,
+            )
+            return bank
+
+        def quantise(grouped, name, tag):
+            codes = keep.tile([P, S], U32, name=name + "_codes", tag=tag, align_bytes=64)
+            scales = keep.tile([P, S], U8, name=name + "_scales", align_bytes=64)
+            nc.vector.quantize_mx(codes[:].bitcast(FP8X4), scales[:], grouped[:].rearrange("p c t -> p (c t)"))
+            return codes, scales
+
+        table_scales = cleared(x_scales, "table_scales")
+        w1_rows = cleared(w1_scales, "w1_rows")
+        w2_rows = cleared(w2_scales, "w2_rows")
+        warm = keep.tile([P, 2], F32, name="warm")
+        nc.vector.memset(warm[:, 0:1], 0.0)
+        nc.scalar.activation(warm[:, 1:2], warm[:, 0:1], ACT.Sigmoid)
+
+        offs_sb = load_list(offs, "offs_sb")
+        w1_raw = load_weight_words(w1_words, "w1_raw")
+        table_words = keep.tile([P, T], I32, name="table_words")
+        nc.sync.dma_start(table_words[:], x_words[0].rearrange("p c r -> p (c r)").bitcast(I32))
+        load_scale_rows([nc.sync] * 4, table_scales, x_scales)
+        load_scale_rows([nc.sync] * 3 + [nc.gpsimd], w1_rows, w1_scales)
+        n3_sb = load_list(n3, "n3_sb")
+        n4_sb = load_list(n4, "n4_sb")
+        w2_raw = load_weight_words(w2_words, "w2_raw")
+        load_scale_rows([nc.sync] * 4, w2_rows, w2_scales)
+        gain = keep.tile([P, PACK], F32, name="gain")
+        nc.sync.dma_start(gain[:], gn.rearrange("(p t) o -> p (t o)", t=PACK))
+        n1_sb = load_list(n1, "n1_sb")
+        n2_sb = load_list(n2, "n2_sb")
+        n6_sb = load_list(n6, "n6_sb")
+        n5_sb = load_list(n5, "n5_sb")
+
+        w1 = deal(w1_raw, w1_rows, "w1")
+        x_bytes = keep.tile([P, S], U8, name="x_bytes", align_bytes=64)
+        x_codes = keep.tile([P, S], U32, name="x_codes", align_bytes=64)
+        nc.vector.tensor_copy(x_codes[:], table_words[:].bitcast(U32).indirect(offs_sb[:]))
+        nc.vector.tensor_copy(x_bytes[:], table_scales[:].indirect(offs_sb[:]))
+
+        y_banks = [product(w1, x_codes, x_bytes, t, "first") for t in range(PACK)]
+        w2 = deal(w2_raw, w2_rows, "w2")
+        gain75 = keep.tile([P, PACK], F32, name="gain75")
+        nc.vector.tensor_scalar_mul(gain75[:], gain[:], 0.75)
+
+        y = [keep.tile([P, WIDE], F32, name="y" + str(t)) for t in range(PACK)]
+        y43 = keep.tile([P, PACK, S], F32, name="y43")
+
+        def minus_four_thirds(t):
+            nc.scalar.activation(y43[:, t, :], y_banks[t][:], ACT.Copy, scale=-4.0 / 3.0)
+
+        for t in range(PACK):
+            nc.scalar.copy(y[t][:, :S], y_banks[t][:])
+        minus_four_thirds(0)
+
+        def pair_tiles(name):
+            return [keep.tile([P, 2, W], F32, name=name + str(u), tag=name + str(u), align_bytes=64) for u in range(2)]
+
+        pa, pb, lead = pair_tiles("pa"), pair_tiles("pb"), pair_tiles("lead")
+        share_a, share_b = pair_tiles("share_a"), pair_tiles("share_b")
+
+        def fetch_a(t):
+            nc.vector.tensor_copy(pa[t // 2][:, t % 2, :], y[t][:].indirect(n3_sb[:]))
+
+        def fetch_b(t):
+            nc.vector.tensor_copy(pb[t // 2][:, t % 2, :], y[t][:].indirect(n4_sb[:]))
+
+        def shares(u):
+            nc.vector.tensor_tensor(lead[u][:], pb[u][:], pa[u][:], ALU.subtract)
+            nc.scalar.activation(share_a[u][:], lead[u][:], ACT.Sigmoid, scale=-1.0)
+            nc.scalar.activation(share_b[u][:], lead[u][:], ACT.Sigmoid)
+
+        z_grouped = keep.tile([P, S, PACK], BF16, name="z_grouped", align_bytes=64)
+        z2_grouped = keep.tile([P, S, PACK], BF16, name="z2_grouped", tag="z2_grouped", align_bytes=64)
+        duel = [keep.tile([P, S], F32, name="duel" + str(t)) for t in range(PACK)]
+
+        def z_first(t, part):
+            nc.vector.tensor_tensor(part, y[t][:].indirect(n1_sb[:]), y43[:, t, :], ALU.add)
+
+        def z_second(t, part, mixed):
+            nc.vector.tensor_tensor(mixed, y[t][:].indirect(n2_sb[:]), part, ALU.add)
+
+        def z_round(t, mixed):
+            nc.scalar.activation(z_grouped[:, :, t], mixed, ACT.Copy, scale=gain75[:, t : t + 1])
+
+        def scatter_pair(u):
+            for e in range(2):
+                nc.vector.tensor_tensor(duel[2 * u + e][:].indirect(n3_sb[:]), pa[u][:, e, :], share_a[u][:, e, :], ALU.mult)
+            for e in range(2):
+                t = 2 * u + e
+                nc.vector.tensor_tensor(duel[t][:].indirect(n4_sb[:]), pb[u][:, e, :], share_b[u][:, e, :], ALU.mult)
+                nc.scalar.activation(z2_grouped[:, :, t], duel[t][:], ACT.Copy, scale=gain[:, t : t + 1])
+
+        fetch_a(0)
+        fetch_b(0)
+        fetch_a(1)
+        fetch_b(1)
+        fetch_a(2)
+        shares(0)
+        fetch_b(2)
+        fetch_a(3)
+        fetch_b(3)
+        part0 = keep.tile([P, S], F32, name="part0")
+        z_first(0, part0[:])
+        shares(1)
+        for t in range(1, PACK):
+            minus_four_thirds(t)
+        nc.scalar.activation(warm[:, 1:2], share_b[1][:, 1, 0:1], ACT.Abs_reciprocal_sqrt)
+        scatter_pair(0)
+        scatter_pair(1)
+
+        part1 = keep.tile([P, S], F32, name="part1", tag="pa1", align_bytes=64)
+        mixed0 = keep.tile([P, S], F32, name="mixed0", tag="share_a1", align_bytes=64)
+        mixed1 = keep.tile([P, S], F32, name="mixed1")
+        z_first(1, part1[:])
+        z_second(0, part0[:], mixed0[:])
+        z2_codes, z2_scales = quantise(z2_grouped, "z2", "z2_codes")
+        z_round(0, mixed0[:])
+        late = keep.tile([P, 4, S], F32, name="late", tag="z2_grouped", align_bytes=64)
+
+        b_banks = [product(w2, z2_codes, z2_scales, t, "second") for t in range(PACK)]
+        b_abs = [keep.tile([P, WIDE], F32, name="b_abs" + str(t)) for t in range(PACK)]
+        b_own = [keep.tile([P, S], F32, name="b_own" + str(t), tag="b_own" + str(t), align_bytes=64) for t in range(PACK)]
+        for t in range(PACK):
+            nc.scalar.activation(b_abs[t][:, :S], b_banks[t][:], ACT.Abs)
+            nc.sync.dma_start(b_own[t][:], b_abs[t][:, :S])
+
+        z_second(1, part1[:], mixed1[:])
+        z_round(1, mixed1[:])
+        z_first(2, late[:, 0, :])
+        z_first(3, late[:, 1, :])
+        for t in (2, 3):
+            z_second(t, late[:, t - 2, :], late[:, t, :])
+            z_round(t, late[:, t, :])
+
+        den = keep.tile([P, PACK, S], F32, name="den")
+        rec = keep.tile([P, PACK, S], F32, name="rec")
+
+        def denominator(t):
+            nc.vector.tensor_tensor(den[:, t, :], b_abs[t][:].indirect(n6_sb[:]), b_own[t][:], ALU.add)
+
+        def inverse_root(t, root):
+            nc.scalar.activation(root, den[:, t, :], ACT.Abs_reciprocal_sqrt, bias=0.5)
+
+        def square(t, root):
+            nc.scalar.activation(rec[:, t, :], root, ACT.Square)
+
+        denominator(0)
+        denominator(1)
+        z_codes, z_scales = quantise(z_grouped, "z", "b_own0")
+        denominator(2)
+        denominator(3)
+        root0 = keep.tile([P, S], F32, name="root0")
+        inverse_root(0, root0[:])
+        square(0, root0[:])
+        a_banks = [product(w2, z_codes, z_scales, t, "first") for t in range(PACK)]
+        a_neg = [keep.tile([P, WIDE], F32, name="a_neg" + str(t)) for t in range(PACK)]
+        a_own = [keep.tile([P, S], F32, name="a_own" + str(t), tag="a_own" + str(t)) for t in range(PACK)]
+        for t in range(PACK):
+            nc.scalar.activation(a_neg[t][:, :S], a_banks[t][:], ACT.Copy, scale=-1.0)
+            nc.scalar.copy(a_own[t][:], a_banks[t][:])
+
+        num = keep.tile([P, PACK, S], F32, name="num")
+        res = keep.tile([P, PACK, S], F32, name="res")
+        out_rows = out_0.rearrange("(p t) c -> p t c", t=PACK)
+
+        def numerator(t):
+            nc.vector.tensor_tensor(num[:, t, :], a_neg[t][:].indirect(n5_sb[:]), a_own[t][:], ALU.add)
+
+        def result(t):
+            nc.vector.tensor_tensor(res[:, t, :], num[:, t, :], rec[:, t, :], ALU.mult)
+            nc.sync.dma_start(out_rows[:, t, :], res[:, t, :])
+
+        numerator(0)
+        roots = keep.tile([P, 3, S], F32, name="roots", tag="a_own0")
+        inverse_root(1, roots[:, 0, :])
+        inverse_root(2, roots[:, 1, :])
+        square(1, roots[:, 0, :])
+        inverse_root(3, roots[:, 2, :])
+        square(2, roots[:, 1, :])
+        square(3, roots[:, 2, :])
+        numerator(1)
+        numerator(2)
+        result(0)
+        numerator(3)
+        for t in range(1, PACK):
+            result(t)
+
+        out_codes = keep.tile([P, S], I32, name="out_codes", align_bytes=64)
+        out_scales = keep.tile([P, S], U8, name="out_scales", align_bytes=64)
+        out_words = out_1[0].rearrange("p c r -> p (c r)").bitcast(I32)
+        res_grouped = [keep.tile([P, HALF, PACK], BF16, name="res_grouped" + str(h), align_bytes=64) for h in range(2)]
+        for h in range(2):
+            cols = slice(h * HALF, (h + 1) * HALF)
+            nc.vector.tensor_copy(res_grouped[h][:], res[:, :, cols].rearrange("p t c -> p c t"))
+        for h in range(2):
+            cols = slice(h * HALF, (h + 1) * HALF)
+            nc.vector.quantize_mx(
+                out_codes[:, cols].bitcast(FP8X4), out_scales[:, cols], res_grouped[h][:].rearrange("p c t -> p (c t)")
+            )
+            nc.scalar.dma_start(out_words[:, cols], out_codes[:, cols])
+        for q in range(4):
+            queue = nc.sync if q % 2 == 0 else nc.scalar
+            queue.dma_start(out_2[0, 4 * q : 4 * q + 4, :].bitcast(I32), out_scales[32 * q : 32 * q + 4, :].bitcast(I32))

@@ -63,14 +63,14 @@ def tile_picked_tienormblapduel_none_po_kernel(
             )
             return dealt_words, dealt_scales
 
-        def product(weight, codes, scales, t, tag):
-            bank = psum.tile([P, S], F32, name=tag + str(t), tag=tag + str(t))
+        def product(weight, codes, scales, t, tag, cols):
+            bank = psum.tile([P, cols.stop - cols.start], F32, name=tag + str(t), tag=tag + str(t))
             nc.tensor.matmul_mx(
                 bank[:],
                 lhsT=weight[0][:, 2 * P * t : 2 * P * (t + 1)].bitcast(FP4X4),
                 lhsT_scale=weight[1][:, P * t : P * (t + 1)],
-                rhs=codes[:].bitcast(FP8X4),
-                rhs_scale=scales[:],
+                rhs=codes[:, cols].bitcast(FP8X4),
+                rhs_scale=scales[:, cols],
                 start=True,
                 stop=True,
             )
@@ -86,14 +86,12 @@ def tile_picked_tienormblapduel_none_po_kernel(
         w1_rows = cleared(w1_scales, "w1_rows")
         w2_rows = cleared(w2_scales, "w2_rows")
         warm = keep.tile([P, 2], F32, name="warm")
-        nc.vector.memset(warm[:, 0:1], 0.0)
-        nc.scalar.activation(warm[:, 1:2], warm[:, 0:1], ACT.Sigmoid)
 
         offs_sb = load_list(offs, "offs_sb")
         w1_raw = load_weight_words(w1_words, "w1_raw")
         table_words = keep.tile([P, T], I32, name="table_words")
         nc.sync.dma_start(table_words[:], x_words[0].rearrange("p c r -> p (c r)").bitcast(I32))
-        load_scale_rows([nc.sync] * 4, table_scales, x_scales)
+        load_scale_rows([nc.scalar] * 4, table_scales, x_scales)
         load_scale_rows([nc.sync] * 3 + [nc.gpsimd], w1_rows, w1_scales)
         n3_sb = load_list(n3, "n3_sb")
         n4_sb = load_list(n4, "n4_sb")
@@ -109,23 +107,28 @@ def tile_picked_tienormblapduel_none_po_kernel(
         w1 = deal(w1_raw, w1_rows, "w1")
         x_bytes = keep.tile([P, S], U8, name="x_bytes", align_bytes=64)
         x_codes = keep.tile([P, S], U32, name="x_codes", align_bytes=64)
-        nc.vector.tensor_copy(x_codes[:], table_words[:].bitcast(U32).indirect(offs_sb[:]))
         nc.vector.tensor_copy(x_bytes[:], table_scales[:].indirect(offs_sb[:]))
+        halves = [slice(0, HALF), slice(HALF, S)]
+        for h in range(2):
+            nc.vector.tensor_copy(
+                x_codes[:, halves[h]], table_words[:].bitcast(U32).indirect(offs_sb[:, 16 * h : 16 * (h + 1)])
+            )
 
-        y_banks = [product(w1, x_codes, x_bytes, t, "first") for t in range(PACK)]
+        y_parts = [[(product(w1, x_codes, x_bytes, 0, tag, cols), cols) for tag, cols in zip(("first", "second"), halves)]]
+        for t in range(1, PACK):
+            y_parts.append([(product(w1, x_codes, x_bytes, t, "first", slice(0, S)), slice(0, S))])
         w2 = deal(w2_raw, w2_rows, "w2")
         gain75 = keep.tile([P, PACK], F32, name="gain75")
         nc.vector.tensor_scalar_mul(gain75[:], gain[:], 0.75)
+        gain_neg = keep.tile([P, PACK], F32, name="gain_neg")
+        nc.vector.tensor_scalar_mul(gain_neg[:], gain[:], -1.0)
 
-        y = [keep.tile([P, WIDE], F32, name="y" + str(t)) for t in range(PACK)]
-        y43 = keep.tile([P, PACK, S], F32, name="y43")
-
-        def minus_four_thirds(t):
-            nc.scalar.activation(y43[:, t, :], y_banks[t][:], ACT.Copy, scale=-4.0 / 3.0)
-
+        y = [keep.tile([P, S], F32, name="y" + str(t)) for t in range(PACK)]
+        y75 = [keep.tile([P, WIDE], F32, name="y75_" + str(t)) for t in range(PACK)]
+        y_neg = keep.tile([P, PACK, S], F32, name="y_neg")
         for t in range(PACK):
-            nc.scalar.copy(y[t][:, :S], y_banks[t][:])
-        minus_four_thirds(0)
+            for bank, cols in y_parts[t]:
+                nc.scalar.copy(y[t][:, cols], bank[:])
 
         def pair_tiles(name):
             return [keep.tile([P, 2, W], F32, name=name + str(u), tag=name + str(u), align_bytes=64) for u in range(2)]
@@ -149,21 +152,22 @@ def tile_picked_tienormblapduel_none_po_kernel(
         duel = [keep.tile([P, S], F32, name="duel" + str(t)) for t in range(PACK)]
 
         def z_first(t, part):
-            nc.vector.tensor_tensor(part, y[t][:].indirect(n1_sb[:]), y43[:, t, :], ALU.add)
+            nc.vector.tensor_tensor(part, y75[t][:].indirect(n1_sb[:]), y_neg[:, t, :], ALU.add)
 
         def z_second(t, part, mixed):
-            nc.vector.tensor_tensor(mixed, y[t][:].indirect(n2_sb[:]), part, ALU.add)
+            nc.vector.tensor_tensor(mixed, y75[t][:].indirect(n2_sb[:]), part, ALU.add)
 
-        def z_round(t, mixed):
-            nc.scalar.activation(z_grouped[:, :, t], mixed, ACT.Copy, scale=gain75[:, t : t + 1])
+        def z_round(u, pair):
+            nc.scalar.copy(z_grouped[:, :, 2 * u : 2 * u + 2], pair.rearrange("p e c -> p c e"))
 
-        def scatter_pair(u):
-            for e in range(2):
-                nc.vector.tensor_tensor(duel[2 * u + e][:].indirect(n3_sb[:]), pa[u][:, e, :], share_a[u][:, e, :], ALU.mult)
-            for e in range(2):
-                t = 2 * u + e
-                nc.vector.tensor_tensor(duel[t][:].indirect(n4_sb[:]), pb[u][:, e, :], share_b[u][:, e, :], ALU.mult)
-                nc.scalar.activation(z2_grouped[:, :, t], duel[t][:], ACT.Copy, scale=gain[:, t : t + 1])
+        def scatter_a(t):
+            u, e = divmod(t, 2)
+            nc.vector.tensor_tensor(duel[t][:].indirect(n3_sb[:]), pa[u][:, e, :], share_a[u][:, e, :], ALU.mult)
+
+        def scatter_b(t):
+            u, e = divmod(t, 2)
+            nc.vector.tensor_tensor(duel[t][:].indirect(n4_sb[:]), pb[u][:, e, :], share_b[u][:, e, :], ALU.mult)
+            nc.scalar.activation(z2_grouped[:, :, t], duel[t][:], ACT.Copy, scale=gain[:, t : t + 1])
 
         fetch_a(0)
         fetch_b(0)
@@ -174,38 +178,44 @@ def tile_picked_tienormblapduel_none_po_kernel(
         fetch_b(2)
         fetch_a(3)
         fetch_b(3)
-        part0 = keep.tile([P, S], F32, name="part0")
-        z_first(0, part0[:])
+        scatter_a(0)
         shares(1)
-        for t in range(1, PACK):
-            minus_four_thirds(t)
         nc.scalar.activation(warm[:, 1:2], share_b[1][:, 1, 0:1], ACT.Abs_reciprocal_sqrt)
-        scatter_pair(0)
-        scatter_pair(1)
+        for t in range(PACK):
+            for bank, cols in y_parts[t]:
+                nc.scalar.activation(y75[t][:, cols], bank[:], ACT.Copy, scale=gain75[:, t : t + 1])
+                nc.scalar.activation(y_neg[:, t, cols], bank[:], ACT.Copy, scale=gain_neg[:, t : t + 1])
+        scatter_a(1)
+        scatter_b(0)
+        scatter_b(1)
+        scatter_a(2)
+        scatter_a(3)
+        scatter_b(2)
+        scatter_b(3)
 
-        part1 = keep.tile([P, S], F32, name="part1", tag="pa1", align_bytes=64)
-        mixed0 = keep.tile([P, S], F32, name="mixed0", tag="share_a1", align_bytes=64)
-        mixed1 = keep.tile([P, S], F32, name="mixed1")
+        part0 = keep.tile([P, S], F32, name="part0", tag="pa1", align_bytes=64)
+        part1 = keep.tile([P, S], F32, name="part1", tag="share_a1", align_bytes=64)
+        early = keep.tile([P, 2, S], F32, name="early")
+        z_first(0, part0[:])
         z_first(1, part1[:])
-        z_second(0, part0[:], mixed0[:])
         z2_codes, z2_scales = quantise(z2_grouped, "z2", "z2_codes")
-        z_round(0, mixed0[:])
+        z_second(0, part0[:], early[:, 0, :])
+        z_second(1, part1[:], early[:, 1, :])
         late = keep.tile([P, 4, S], F32, name="late", tag="z2_grouped", align_bytes=64)
 
-        b_banks = [product(w2, z2_codes, z2_scales, t, "second") for t in range(PACK)]
+        b_banks = [product(w2, z2_codes, z2_scales, t, "second", slice(0, S)) for t in range(PACK)]
         b_abs = [keep.tile([P, WIDE], F32, name="b_abs" + str(t)) for t in range(PACK)]
         b_own = [keep.tile([P, S], F32, name="b_own" + str(t), tag="b_own" + str(t), align_bytes=64) for t in range(PACK)]
         for t in range(PACK):
             nc.scalar.activation(b_abs[t][:, :S], b_banks[t][:], ACT.Abs)
             nc.sync.dma_start(b_own[t][:], b_abs[t][:, :S])
 
-        z_second(1, part1[:], mixed1[:])
-        z_round(1, mixed1[:])
+        z_round(0, early[:])
         z_first(2, late[:, 0, :])
         z_first(3, late[:, 1, :])
         for t in (2, 3):
             z_second(t, late[:, t - 2, :], late[:, t, :])
-            z_round(t, late[:, t, :])
+        z_round(1, late[:, 2:4, :])
 
         den = keep.tile([P, PACK, S], F32, name="den")
         rec = keep.tile([P, PACK, S], F32, name="rec")
@@ -224,10 +234,12 @@ def tile_picked_tienormblapduel_none_po_kernel(
         z_codes, z_scales = quantise(z_grouped, "z", "b_own0")
         denominator(2)
         denominator(3)
-        root0 = keep.tile([P, S], F32, name="root0")
-        inverse_root(0, root0[:])
-        square(0, root0[:])
-        a_banks = [product(w2, z_codes, z_scales, t, "first") for t in range(PACK)]
+        first_roots = keep.tile([P, 2, S], F32, name="first_roots")
+        for t in range(2):
+            inverse_root(t, first_roots[:, t, :])
+        for t in range(2):
+            square(t, first_roots[:, t, :])
+        a_banks = [product(w2, z_codes, z_scales, t, "first", slice(0, S)) for t in range(PACK)]
         a_neg = [keep.tile([P, WIDE], F32, name="a_neg" + str(t)) for t in range(PACK)]
         a_own = [keep.tile([P, S], F32, name="a_own" + str(t), tag="a_own" + str(t)) for t in range(PACK)]
         for t in range(PACK):
@@ -246,31 +258,31 @@ def tile_picked_tienormblapduel_none_po_kernel(
             nc.sync.dma_start(out_rows[:, t, :], res[:, t, :])
 
         numerator(0)
-        roots = keep.tile([P, 3, S], F32, name="roots", tag="a_own0")
-        inverse_root(1, roots[:, 0, :])
-        inverse_root(2, roots[:, 1, :])
-        square(1, roots[:, 0, :])
-        inverse_root(3, roots[:, 2, :])
-        square(2, roots[:, 1, :])
-        square(3, roots[:, 2, :])
+        last_roots = keep.tile([P, 2, S], F32, name="last_roots", tag="a_own0")
+        for t in (2, 3):
+            inverse_root(t, last_roots[:, t - 2, :])
+        for t in (2, 3):
+            square(t, last_roots[:, t - 2, :])
         numerator(1)
         numerator(2)
         result(0)
         numerator(3)
-        for t in range(1, PACK):
-            result(t)
+        result(1)
+        res_grouped = keep.tile([P, S, PACK], BF16, name="res_grouped", align_bytes=64)
+        nc.scalar.copy(res_grouped[:, :, 0:2], res[:, 0:2, :].rearrange("p e c -> p c e"))
+        result(2)
+        result(3)
 
         out_codes = keep.tile([P, S], I32, name="out_codes", align_bytes=64)
         out_scales = keep.tile([P, S], U8, name="out_scales", align_bytes=64)
         out_words = out_1[0].rearrange("p c r -> p (c r)").bitcast(I32)
-        res_grouped = [keep.tile([P, HALF, PACK], BF16, name="res_grouped" + str(h), align_bytes=64) for h in range(2)]
         for h in range(2):
             cols = slice(h * HALF, (h + 1) * HALF)
-            nc.vector.tensor_copy(res_grouped[h][:], res[:, :, cols].rearrange("p t c -> p c t"))
+            nc.vector.tensor_copy(res_grouped[:, cols, 2:4], res[:, 2:4, cols].rearrange("p e c -> p c e"))
         for h in range(2):
             cols = slice(h * HALF, (h + 1) * HALF)
             nc.vector.quantize_mx(
-                out_codes[:, cols].bitcast(FP8X4), out_scales[:, cols], res_grouped[h][:].rearrange("p c t -> p (c t)")
+                out_codes[:, cols].bitcast(FP8X4), out_scales[:, cols], res_grouped[:, cols, :].rearrange("p c t -> p (c t)")
             )
             nc.scalar.dma_start(out_words[:, cols], out_codes[:, cols])
         for q in range(4):

@@ -50,17 +50,24 @@ def tile_picked_tienormblapduel_none_po_kernel(
             nc.sync.dma_start(tile[:].bitcast(I32), src[0].bitcast(I32))
             return tile
 
-        def deal(words, scales, name):
+        def scale_engine_is_split(name):
+            return name == "w1"
+
+        def deal(words, scales, scale_engine, name):
             dealt_words = keep.tile([P, 2 * H], U8, name=name + "_words", align_bytes=64)
             dealt_scales = keep.tile([P, H], U8, name=name + "_scales", align_bytes=64)
             nc.vector.tensor_copy(
                 dealt_words[:].rearrange("p (t m b) -> p t m b", t=PACK, b=2),
                 words[:].rearrange("p (m t b) -> p t m b", t=PACK, b=2),
             )
-            nc.vector.tensor_copy(
-                dealt_scales[:].rearrange("p (t m) -> p t m", t=PACK),
-                scales[:].rearrange("p (m t) -> p t m", t=PACK),
-            )
+            if scale_engine_is_split(name):
+                for t in range(PACK):
+                    scale_engine.tensor_copy(dealt_scales[:, P * t : P * (t + 1)], scales[:, t::PACK])
+            else:
+                scale_engine.tensor_copy(
+                    dealt_scales[:].rearrange("p (t m) -> p t m", t=PACK),
+                    scales[:].rearrange("p (m t) -> p t m", t=PACK),
+                )
             return dealt_words, dealt_scales
 
         def product(weight, codes, scales, t, tag, cols):
@@ -82,17 +89,19 @@ def tile_picked_tienormblapduel_none_po_kernel(
             nc.vector.quantize_mx(codes[:].bitcast(FP8X4), scales[:], grouped[:].rearrange("p c t -> p (c t)"))
             return codes, scales
 
-        table_scales = cleared(x_scales, "table_scales")
         w1_rows = cleared(w1_scales, "w1_rows")
+        table_scales = cleared(x_scales, "table_scales")
         w2_rows = cleared(w2_scales, "w2_rows")
         warm = keep.tile([P, 2], F32, name="warm")
+        nc.vector.memset(warm[:, 0:1], 0.0)
 
         offs_sb = load_list(offs, "offs_sb")
         w1_raw = load_weight_words(w1_words, "w1_raw")
         table_words = keep.tile([P, T], I32, name="table_words")
         nc.sync.dma_start(table_words[:], x_words[0].rearrange("p c r -> p (c r)").bitcast(I32))
-        load_scale_rows([nc.scalar] * 4, table_scales, x_scales)
-        load_scale_rows([nc.sync] * 3 + [nc.gpsimd], w1_rows, w1_scales)
+        load_scale_rows([nc.gpsimd] + [nc.sync] * 3, w1_rows, w1_scales)
+        load_scale_rows([nc.sync] * 4, table_scales, x_scales)
+        nc.scalar.activation(warm[:, 1:2], warm[:, 0:1], ACT.Sigmoid)
         n3_sb = load_list(n3, "n3_sb")
         n4_sb = load_list(n4, "n4_sb")
         w2_raw = load_weight_words(w2_words, "w2_raw")
@@ -104,24 +113,22 @@ def tile_picked_tienormblapduel_none_po_kernel(
         n6_sb = load_list(n6, "n6_sb")
         n5_sb = load_list(n5, "n5_sb")
 
-        w1 = deal(w1_raw, w1_rows, "w1")
+        w1 = deal(w1_raw, w1_rows, nc.gpsimd, "w1")
         x_bytes = keep.tile([P, S], U8, name="x_bytes", align_bytes=64)
         x_codes = keep.tile([P, S], U32, name="x_codes", align_bytes=64)
-        nc.vector.tensor_copy(x_bytes[:], table_scales[:].indirect(offs_sb[:]))
+        nc.vector.tensor_copy(x_codes[:], table_words[:].bitcast(U32).indirect(offs_sb[:]))
         halves = [slice(0, HALF), slice(HALF, S)]
         for h in range(2):
-            nc.vector.tensor_copy(
-                x_codes[:, halves[h]], table_words[:].bitcast(U32).indirect(offs_sb[:, 16 * h : 16 * (h + 1)])
-            )
+            nc.vector.tensor_copy(x_bytes[:, halves[h]], table_scales[:].indirect(offs_sb[:, 16 * h : 16 * (h + 1)]))
 
         y_parts = [[(product(w1, x_codes, x_bytes, 0, tag, cols), cols) for tag, cols in zip(("first", "second"), halves)]]
         for t in range(1, PACK):
             y_parts.append([(product(w1, x_codes, x_bytes, t, "first", slice(0, S)), slice(0, S))])
-        w2 = deal(w2_raw, w2_rows, "w2")
+        w2 = deal(w2_raw, w2_rows, nc.vector, "w2")
         gain75 = keep.tile([P, PACK], F32, name="gain75")
-        nc.vector.tensor_scalar_mul(gain75[:], gain[:], 0.75)
+        nc.scalar.activation(gain75[:], gain[:], ACT.Copy, scale=0.75)
         gain_neg = keep.tile([P, PACK], F32, name="gain_neg")
-        nc.vector.tensor_scalar_mul(gain_neg[:], gain[:], -1.0)
+        nc.scalar.activation(gain_neg[:], gain[:], ACT.Copy, scale=-1.0)
 
         y = [keep.tile([P, S], F32, name="y" + str(t)) for t in range(PACK)]
         y75 = [keep.tile([P, WIDE], F32, name="y75_" + str(t)) for t in range(PACK)]
@@ -142,8 +149,11 @@ def tile_picked_tienormblapduel_none_po_kernel(
         def fetch_b(t):
             nc.vector.tensor_copy(pb[t // 2][:, t % 2, :], y[t][:].indirect(n4_sb[:]))
 
+        def difference(engine, t):
+            u, e = divmod(t, 2)
+            engine.tensor_tensor(lead[u][:, e, :], pb[u][:, e, :], pa[u][:, e, :], ALU.subtract)
+
         def shares(u):
-            nc.vector.tensor_tensor(lead[u][:], pb[u][:], pa[u][:], ALU.subtract)
             nc.scalar.activation(share_a[u][:], lead[u][:], ACT.Sigmoid, scale=-1.0)
             nc.scalar.activation(share_b[u][:], lead[u][:], ACT.Sigmoid)
 
@@ -169,16 +179,15 @@ def tile_picked_tienormblapduel_none_po_kernel(
             nc.vector.tensor_tensor(duel[t][:].indirect(n4_sb[:]), pb[u][:, e, :], share_b[u][:, e, :], ALU.mult)
             nc.scalar.activation(z2_grouped[:, :, t], duel[t][:], ACT.Copy, scale=gain[:, t : t + 1])
 
-        fetch_a(0)
-        fetch_b(0)
-        fetch_a(1)
-        fetch_b(1)
-        fetch_a(2)
-        shares(0)
-        fetch_b(2)
-        fetch_a(3)
-        fetch_b(3)
+        for t in range(PACK):
+            fetch_a(t)
+            fetch_b(t)
+            if t < PACK - 1:
+                difference(nc.gpsimd, t)
+            if t == 1:
+                shares(0)
         scatter_a(0)
+        difference(nc.vector, PACK - 1)
         shares(1)
         nc.scalar.activation(warm[:, 1:2], share_b[1][:, 1, 0:1], ACT.Abs_reciprocal_sqrt)
         for t in range(PACK):
@@ -208,7 +217,10 @@ def tile_picked_tienormblapduel_none_po_kernel(
         b_own = [keep.tile([P, S], F32, name="b_own" + str(t), tag="b_own" + str(t), align_bytes=64) for t in range(PACK)]
         for t in range(PACK):
             nc.scalar.activation(b_abs[t][:, :S], b_banks[t][:], ACT.Abs)
-            nc.sync.dma_start(b_own[t][:], b_abs[t][:, :S])
+            if t < 2:
+                nc.scalar.activation(b_own[t][:], b_banks[t][:], ACT.Abs)
+            else:
+                nc.sync.dma_start(b_own[t][:], b_abs[t][:, :S])
 
         z_round(0, early[:])
         z_first(2, late[:, 0, :])
@@ -264,12 +276,13 @@ def tile_picked_tienormblapduel_none_po_kernel(
         for t in (2, 3):
             square(t, last_roots[:, t - 2, :])
         numerator(1)
-        numerator(2)
         result(0)
-        numerator(3)
+        numerator(2)
         result(1)
-        res_grouped = keep.tile([P, S, PACK], BF16, name="res_grouped", align_bytes=64)
-        nc.scalar.copy(res_grouped[:, :, 0:2], res[:, 0:2, :].rearrange("p e c -> p c e"))
+        numerator(3)
+        res_grouped = [keep.tile([P, HALF, PACK], BF16, name="res_grouped" + str(h), align_bytes=64) for h in range(2)]
+        for h in range(2):
+            nc.scalar.copy(res_grouped[h][:, :, 0:2], res[:, 0:2, halves[h]].rearrange("p e c -> p c e"))
         result(2)
         result(3)
 
@@ -278,11 +291,11 @@ def tile_picked_tienormblapduel_none_po_kernel(
         out_words = out_1[0].rearrange("p c r -> p (c r)").bitcast(I32)
         for h in range(2):
             cols = slice(h * HALF, (h + 1) * HALF)
-            nc.vector.tensor_copy(res_grouped[:, cols, 2:4], res[:, 2:4, cols].rearrange("p e c -> p c e"))
+            nc.vector.tensor_copy(res_grouped[h][:, :, 2:4], res[:, 2:4, cols].rearrange("p e c -> p c e"))
         for h in range(2):
             cols = slice(h * HALF, (h + 1) * HALF)
             nc.vector.quantize_mx(
-                out_codes[:, cols].bitcast(FP8X4), out_scales[:, cols], res_grouped[:, cols, :].rearrange("p c t -> p (c t)")
+                out_codes[:, cols].bitcast(FP8X4), out_scales[:, cols], res_grouped[h][:].rearrange("p c t -> p (c t)")
             )
             nc.scalar.dma_start(out_words[:, cols], out_codes[:, cols])
         for q in range(4):

from contextlib import ExitStack

import concourse.mybir as mybir

K, T, S, H, W = 512, 2048, 512, 512, 256
FLOPS = 3 * 2 * 512 * 512 * 512

F32 = mybir.dt.float32
BF16 = mybir.dt.bfloat16
I32 = mybir.dt.int32
U32 = mybir.dt.uint32
U16 = mybir.dt.uint16
U8 = mybir.dt.uint8
FP8X4 = mybir.dt.float8_e4m3fn_x4
FP4X4 = mybir.dt.float4_e2m1fn_x4
ACT = mybir.ActivationFunctionType
ALU = mybir.AluOpType

P = 128
PACK = 4
HALF = S // 2
WIDE = 2 * S


def tile_picked_tienormblapduel_none_po_kernel(
    tc, x_words, x_scales, w1_words, w1_scales, gn, w2_words, w2_scales, offs, n1, n2, n3, n4, n5, n6, out_0, out_1, out_2
):
    nc = tc.nc
    with ExitStack() as ctx:
        lists = ctx.enter_context(tc.tile_pool(name="lists", bufs=1))
        keep = ctx.enter_context(tc.tile_pool(name="keep", bufs=1))
        psum = ctx.enter_context(tc.psum_pool(name="psum", bufs=1))

        def load_list(src, name):
            tile = lists.tile([P, src.shape[1]], U16, name=name)
            nc.sync.dma_start(tile[:], src)
            return tile

        def cleared(src, name):
            tile = keep.tile([P, src.shape[2]], U8, name=name, align_bytes=64)
            nc.vector.memset(tile[:].bitcast(I32), 0)
            return tile

        def load_scale_rows(queues, tile, src):
            for q in range(4):
                queues[q].dma_start(tile[32 * q : 32 * q + 4, :].bitcast(I32), src[0, 4 * q : 4 * q + 4, :].bitcast(I32))

        def load_weight_words(src, name):
            tile = keep.tile([P, 2 * H], U8, name=name, align_bytes=64)
            nc.sync.dma_start(tile[:].bitcast(I32), src[0].bitcast(I32))
            return tile

        def scale_engine_is_split(name):
            return name == "w1"

        def deal(words, scales, scale_engine, name):
            dealt_words = keep.tile([P, 2 * H], U8, name=name + "_words", align_bytes=64)
            dealt_scales = keep.tile([P, H], U8, name=name + "_scales", align_bytes=64)
            nc.vector.tensor_copy(
                dealt_words[:].rearrange("p (t m b) -> p t m b", t=PACK, b=2),
                words[:].rearrange("p (m t b) -> p t m b", t=PACK, b=2),
            )
            if scale_engine_is_split(name):
                for t in range(PACK):
                    scale_engine.tensor_copy(dealt_scales[:, P * t : P * (t + 1)], scales[:, t::PACK])
            else:
                scale_engine.tensor_copy(
                    dealt_scales[:].rearrange("p (t m) -> p t m", t=PACK),
                    scales[:].rearrange("p (m t) -> p t m", t=PACK),
                )
            return dealt_words, dealt_scales

        def product(weight, codes, scales, t, tag, cols):
            bank = psum.tile([P, cols.stop - cols.start], F32, name=tag + str(t), tag=tag + str(t))
            nc.tensor.matmul_mx(
                bank[:],
                lhsT=weight[0][:, 2 * P * t : 2 * P * (t + 1)].bitcast(FP4X4),
                lhsT_scale=weight[1][:, P * t : P * (t + 1)],
                rhs=codes[:, cols].bitcast(FP8X4),
                rhs_scale=scales[:, cols],
                start=True,
                stop=True,
            )
            return bank

        def quantise(grouped, name, tag):
            codes = keep.tile([P, S], U32, name=name + "_codes", tag=tag, align_bytes=64)
            scales = keep.tile([P, S], U8, name=name + "_scales", align_bytes=64)
            nc.vector.quantize_mx(codes[:].bitcast(FP8X4), scales[:], grouped[:].rearrange("p c t -> p (c t)"))
            return codes, scales

        w1_rows = cleared(w1_scales, "w1_rows")
        table_scales = cleared(x_scales, "table_scales")
        w2_rows = cleared(w2_scales, "w2_rows")
        warm = keep.tile([P, 2], F32, name="warm")
        nc.vector.memset(warm[:, 0:1], 0.0)

        offs_sb = load_list(offs, "offs_sb")
        w1_raw = load_weight_words(w1_words, "w1_raw")
        table_words = keep.tile([P, T], I32, name="table_words")
        nc.sync.dma_start(table_words[:], x_words[0].rearrange("p c r -> p (c r)").bitcast(I32))
        load_scale_rows([nc.gpsimd] + [nc.sync] * 3, w1_rows, w1_scales)
        load_scale_rows([nc.sync] * 4, table_scales, x_scales)
        nc.scalar.activation(warm[:, 1:2], warm[:, 0:1], ACT.Sigmoid)
        n3_sb = load_list(n3, "n3_sb")
        n4_sb = load_list(n4, "n4_sb")
        w2_raw = load_weight_words(w2_words, "w2_raw")
        load_scale_rows([nc.sync] * 4, w2_rows, w2_scales)
        gain = keep.tile([P, PACK], F32, name="gain")
        nc.sync.dma_start(gain[:], gn.rearrange("(p t) o -> p (t o)", t=PACK))
        n1_sb = load_list(n1, "n1_sb")
        n2_sb = load_list(n2, "n2_sb")
        n6_sb = load_list(n6, "n6_sb")
        n5_sb = load_list(n5, "n5_sb")

        w1 = deal(w1_raw, w1_rows, nc.gpsimd, "w1")
        x_bytes = keep.tile([P, S], U8, name="x_bytes", align_bytes=64)
        x_codes = keep.tile([P, S], U32, name="x_codes", align_bytes=64)
        nc.vector.tensor_copy(x_codes[:], table_words[:].bitcast(U32).indirect(offs_sb[:]))
        halves = [slice(0, HALF), slice(HALF, S)]
        for h in range(2):
            nc.vector.tensor_copy(x_bytes[:, halves[h]], table_scales[:].indirect(offs_sb[:, 16 * h : 16 * (h + 1)]))

        y_parts = [[(product(w1, x_codes, x_bytes, 0, tag, cols), cols) for tag, cols in zip(("first", "second"), halves)]]
        for t in range(1, PACK):
            y_parts.append([(product(w1, x_codes, x_bytes, t, "first", slice(0, S)), slice(0, S))])
        w2 = deal(w2_raw, w2_rows, nc.vector, "w2")
        gain75 = keep.tile([P, PACK], F32, name="gain75")
        nc.scalar.activation(gain75[:], gain[:], ACT.Copy, scale=0.75)
        gain_neg = keep.tile([P, PACK], F32, name="gain_neg")
        nc.scalar.activation(gain_neg[:], gain[:], ACT.Copy, scale=-1.0)

        y = [keep.tile([P, S], F32, name="y" + str(t)) for t in range(PACK)]
        y75 = [keep.tile([P, WIDE], F32, name="y75_" + str(t)) for t in range(PACK)]
        y_neg = keep.tile([P, PACK, S], F32, name="y_neg")
        for t in range(PACK):
            for bank, cols in y_parts[t]:
                nc.scalar.copy(y[t][:, cols], bank[:])

        def pair_tiles(name):
            return [keep.tile([P, 2, W], F32, name=name + str(u), tag=name + str(u), align_bytes=64) for u in range(2)]

        pa, pb, lead = pair_tiles("pa"), pair_tiles("pb"), pair_tiles("lead")
        share_a, share_b = pair_tiles("share_a"), pair_tiles("share_b")

        def fetch_a(t):
            nc.vector.tensor_copy(pa[t // 2][:, t % 2, :], y[t][:].indirect(n3_sb[:]))

        def fetch_b(t):
            nc.vector.tensor_copy(pb[t // 2][:, t % 2, :], y[t][:].indirect(n4_sb[:]))

        def difference(engine, t):
            u, e = divmod(t, 2)
            engine.tensor_tensor(lead[u][:, e, :], pb[u][:, e, :], pa[u][:, e, :], ALU.subtract)

        def shares(u):
            nc.scalar.activation(share_a[u][:], lead[u][:], ACT.Sigmoid, scale=-1.0)
            nc.scalar.activation(share_b[u][:], lead[u][:], ACT.Sigmoid)

        z_grouped = keep.tile([P, S, PACK], BF16, name="z_grouped", align_bytes=64)
        z2_grouped = keep.tile([P, S, PACK], BF16, name="z2_grouped", tag="z2_grouped", align_bytes=64)
        duel = [keep.tile([P, S], F32, name="duel" + str(t)) for t in range(PACK)]

        def z_first(t, part):
            nc.vector.tensor_tensor(part, y75[t][:].indirect(n1_sb[:]), y_neg[:, t, :], ALU.add)

        def z_second(t, part, mixed):
            nc.vector.tensor_tensor(mixed, y75[t][:].indirect(n2_sb[:]), part, ALU.add)

        def z_round(u, pair):
            nc.scalar.copy(z_grouped[:, :, 2 * u : 2 * u + 2], pair.rearrange("p e c -> p c e"))

        def scatter_a(t):
            u, e = divmod(t, 2)
            nc.vector.tensor_tensor(duel[t][:].indirect(n3_sb[:]), pa[u][:, e, :], share_a[u][:, e, :], ALU.mult)

        def scatter_b(t):
            u, e = divmod(t, 2)
            nc.vector.tensor_tensor(duel[t][:].indirect(n4_sb[:]), pb[u][:, e, :], share_b[u][:, e, :], ALU.mult)
            nc.scalar.activation(z2_grouped[:, :, t], duel[t][:], ACT.Copy, scale=gain[:, t : t + 1])

        for t in range(PACK):
            fetch_a(t)
            fetch_b(t)
            if t < PACK - 1:
                difference(nc.gpsimd, t)
            if t == 1:
                shares(0)
        scatter_a(0)
        difference(nc.vector, PACK - 1)
        shares(1)
        nc.scalar.activation(warm[:, 1:2], share_b[1][:, 1, 0:1], ACT.Abs_reciprocal_sqrt)
        for t in range(PACK):
            for bank, cols in y_parts[t]:
                nc.scalar.activation(y75[t][:, cols], bank[:], ACT.Copy, scale=gain75[:, t : t + 1])
                nc.scalar.activation(y_neg[:, t, cols], bank[:], ACT.Copy, scale=gain_neg[:, t : t + 1])
        scatter_a(1)
        scatter_b(0)
        scatter_b(1)
        scatter_a(2)
        scatter_a(3)
        scatter_b(2)
        scatter_b(3)

        part0 = keep.tile([P, S], F32, name="part0", tag="pa1", align_bytes=64)
        part1 = keep.tile([P, S], F32, name="part1", tag="share_a1", align_bytes=64)
        early = keep.tile([P, 2, S], F32, name="early")
        z_first(0, part0[:])
        z_first(1, part1[:])
        z2_codes, z2_scales = quantise(z2_grouped, "z2", "z2_codes")
        z_second(0, part0[:], early[:, 0, :])
        z_second(1, part1[:], early[:, 1, :])
        late = keep.tile([P, 4, S], F32, name="late", tag="z2_grouped", align_bytes=64)

        b_banks = [product(w2, z2_codes, z2_scales, t, "second", slice(0, S)) for t in range(PACK)]
        b_abs = [keep.tile([P, WIDE], F32, name="b_abs" + str(t)) for t in range(PACK)]
        b_own = [keep.tile([P, S], F32, name="b_own" + str(t), tag="b_own" + str(t), align_bytes=64) for t in range(PACK)]
        for t in range(PACK):
            nc.scalar.activation(b_abs[t][:, :S], b_banks[t][:], ACT.Abs)
            if t < 2:
                nc.scalar.activation(b_own[t][:], b_banks[t][:], ACT.Abs)
            else:
                nc.sync.dma_start(b_own[t][:], b_abs[t][:, :S])

        z_round(0, early[:])
        z_first(2, late[:, 0, :])
        z_first(3, late[:, 1, :])
        for t in (2, 3):
            z_second(t, late[:, t - 2, :], late[:, t, :])
        z_round(1, late[:, 2:4, :])

        den = keep.tile([P, PACK, S], F32, name="den")
        rec = keep.tile([P, PACK, S], F32, name="rec")

        def denominator(t):
            nc.vector.tensor_tensor(den[:, t, :], b_abs[t][:].indirect(n6_sb[:]), b_own[t][:], ALU.add)

        def inverse_root(t, root):
            nc.scalar.activation(root, den[:, t, :], ACT.Abs_reciprocal_sqrt, bias=0.5)

        def square(t, root):
            nc.scalar.activation(rec[:, t, :], root, ACT.Square)

        denominator(0)
        denominator(1)
        z_codes, z_scales = quantise(z_grouped, "z", "b_own0")
        denominator(2)
        denominator(3)
        first_roots = keep.tile([P, 2, S], F32, name="first_roots")
        for t in range(2):
            inverse_root(t, first_roots[:, t, :])
        for t in range(2):
            square(t, first_roots[:, t, :])
        a_banks = [product(w2, z_codes, z_scales, t, "first", slice(0, S)) for t in range(PACK)]
        a_neg = [keep.tile([P, WIDE], F32, name="a_neg" + str(t)) for t in range(PACK)]
        a_own = [keep.tile([P, S], F32, name="a_own" + str(t), tag="a_own" + str(t)) for t in range(PACK)]
        for t in range(PACK):
            nc.scalar.activation(a_neg[t][:, :S], a_banks[t][:], ACT.Copy, scale=-1.0)
            nc.scalar.copy(a_own[t][:], a_banks[t][:])

        num = keep.tile([P, PACK, S], F32, name="num")
        res = keep.tile([P, PACK, S], F32, name="res")
        out_rows = out_0.rearrange("(p t) c -> p t c", t=PACK)

        def numerator(t):
            nc.vector.tensor_tensor(num[:, t, :], a_neg[t][:].indirect(n5_sb[:]), a_own[t][:], ALU.add)

        def result(t):
            nc.vector.tensor_tensor(res[:, t, :], num[:, t, :], rec[:, t, :], ALU.mult)
            nc.sync.dma_start(out_rows[:, t, :], res[:, t, :])

        numerator(0)
        last_roots = keep.tile([P, 2, S], F32, name="last_roots", tag="a_own0")
        for t in (2, 3):
            inverse_root(t, last_roots[:, t - 2, :])
        for t in (2, 3):
            square(t, last_roots[:, t - 2, :])
        numerator(1)
        result(0)
        numerator(2)
        result(1)
        numerator(3)
        res_grouped = [keep.tile([P, HALF, PACK], BF16, name="res_grouped" + str(h), align_bytes=64) for h in range(2)]
        for h in range(2):
            nc.scalar.copy(res_grouped[h][:, :, 0:2], res[:, 0:2, halves[h]].rearrange("p e c -> p c e"))
        result(2)
        result(3)

        out_codes = keep.tile([P, S], I32, name="out_codes", align_bytes=64)
        out_scales = keep.tile([P, S], U8, name="out_scales", align_bytes=64)
        out_words = out_1[0].rearrange("p c r -> p (c r)").bitcast(I32)
        for h in range(2):
            cols = slice(h * HALF, (h + 1) * HALF)
            nc.vector.tensor_copy(res_grouped[h][:, :, 2:4], res[:, 2:4, cols].rearrange("p e c -> p c e"))
        for h in range(2):
            cols = slice(h * HALF, (h + 1) * HALF)
            nc.vector.quantize_mx(
                out_codes[:, cols].bitcast(FP8X4), out_scales[:, cols], res_grouped[h][:].rearrange("p c t -> p (c t)")
            )
            nc.scalar.dma_start(out_words[:, cols], out_codes[:, cols])
        for q in range(4):
            queue = nc.sync if q % 2 == 0 else nc.scalar
            queue.dma_start(out_2[0, 4 * q : 4 * q + 4, :].bitcast(I32), out_scales[32 * q : 32 * q + 4, :].bitcast(I32))
